import numpy as np, ml_dtypes
CORES = [3,11,19,27,35,43]
N = 6
import mx_ref
BF = ml_dtypes.bfloat16
def gentries(a):
    return np.ascontiguousarray(a.reshape(8, 16, -1).transpose(0, 2, 1)).reshape(8, -1)
def gtable(e):
    e = np.asarray(e); return np.ascontiguousarray(e.reshape(8, -1, 16).transpose(0, 2, 1)).reshape(128, -1).astype(np.int32)
def gcols(t, e):
    v = np.concatenate([t.reshape(8, 16, -1, 4), np.zeros((8, 16, 1, 4), BF)], axis=2)
    return np.ascontiguousarray(np.stack([v[g][:, e[g]] for g in range(8)])).reshape(128, -1)
def f(rng, *shape):
    return mx_ref.flush((rng.standard_normal(shape, dtype=np.float32) * np.exp2(rng.integers(-2, 3, shape[:-1] + (1,)))).astype(BF))
def wide(rng, *shape, cols=0):
    v = rng.standard_normal(shape, dtype=np.float32) * np.exp2(rng.integers(-12, 13, shape)).astype(np.float32)
    if cols: v *= np.repeat(np.exp2(rng.integers(-cols, cols + 1, shape[:-2] + (1, shape[-1] // 4))) * (rng.random(shape[:-2] + (1, shape[-1] // 4)) > 0.0625), 4, axis=-1).astype(np.float32)
    return mx_ref.flush(v.astype(BF))
T, O, K = 128, 2, 256
def lists(rng, alike=False, groups=False, ends=False, few=False):
    c = []
    for r in range(N):
        e = rng.integers(0, K, (8, O, 2, 128))
        if groups: e = np.stack([e[0]] * 8)
        if ends: e = rng.permuted(np.resize([0, K - 1], (8, O, 2, 128)), axis=3)
        if few:
            for m in range(2): e[:, :, m] = rng.permutation(np.resize(rng.permutation(K)[:8], 8 * O * 128)).reshape(8, O, 128)
        c.append(gtable(e.reshape(8, -1)))
    if alike: c = [c[0]] * N
    return np.stack(c)
def setup_inputs(rng):
    return {"x": f(rng, N, 128, 4 * T), "book": np.stack([f(rng, 128, 8 * K)] * N), "cw": lists(rng)}
def setup_inputs_alike(rng):
    d = setup_inputs(rng); d["cw"] = lists(rng, alike=True); return d
def setup_inputs_groups(rng):
    d = setup_inputs(rng); d["cw"] = lists(rng, groups=True); return d
def setup_inputs_ends(rng):
    d = setup_inputs(rng); d["cw"] = lists(rng, ends=True); return d
def setup_inputs_few(rng):
    d = setup_inputs(rng); d["cw"] = lists(rng, few=True); return d
def setup_inputs_spread(rng):
    d = setup_inputs(rng); d["x"] = wide(rng, N, 128, 4 * T, cols=8); d["book"] = np.stack([wide(rng, 128, 8 * K, cols=4)] * N); return d
def check_inputs(d):
    b = []
    for r in range(N):
        if d["cw"][r].min() < 0 or d["cw"][r].max() >= K: b.append("cw")
        if d["book"][r].tobytes() != d["book"][0].tobytes(): b.append("book")
    return b
def reference(x, book, cw):
    W = []
    for s in range(N):
        e = gentries(cw[s])
        for o in range(O):
            a, b = [gcols(np.ascontiguousarray(book[s][:, 4 * K * m:4 * K * m + 4 * K]), e[:, (2 * o + m) * 128:(2 * o + m) * 128 + 128]).astype(np.float32) for m in range(2)]
            W.append(mx_ref.quantize((a + b).astype(BF)))
    y = np.zeros((N, 128, N * O * T), np.float32)
    for r in range(N):
        X = mx_ref.quantize(np.ascontiguousarray(x[r]))
        for i in range(N * O): y[r][:, T * i:T * i + T] = mx_ref.matmul(W[i], X)
    return {"y": y}

@@ -1,0 +1,166 @@
+from concourse.bass import DstId, RemoteDMATransfer
+from concourse.mybir import dt, AluOpType, ActivationFunctionType
+
+N, O, W, K = 6, 2, 128, 256
+P = O * W
+
+SCRATCH = {
+    "cwb": ("sbuf", [128, O, 2, W // 16], "int32"),
+    "b0": ("sbuf", [128, 4 * K], "bfloat16"),
+    "b1": ("sbuf", [128, 4 * K], "bfloat16"),
+    "xb": ("sbuf", [128, 4 * W], "bfloat16"),
+    "qx": ("sbuf", [128, W], "float8_e4m3fn_x4"),
+    "px": ("sbuf", [128, W], "uint8"),
+    "of": ("sbuf", [128, 2 * 4 * P // 16], "uint16"),
+    "yb": ("sbuf", [128, N * P], "float32"),
+}
+SEMAPHORES = ["l_cw", "l_b0", "l_b1", "l_x", "ofa", "ofb", "v_qx", "sent_l", "sent_c", "stored"]
+for _s in range(N):
+    SCRATCH["L%d" % _s] = ("sbuf", [128, 2 * 4 * P // 16], "uint16")
+    SCRATCH["a%d" % _s] = ("sbuf", [128, 4 * P], "bfloat16")
+    SCRATCH["h%d" % _s] = ("sbuf", [128, 4 * P], "bfloat16")
+    SCRATCH["q%d" % _s] = ("sbuf", [128, P], "float8_e4m3fn_x4")
+    SCRATCH["p%d" % _s] = ("sbuf", [128, P], "uint8")
+    SEMAPHORES += ["arrl%d" % _s, "arrc%d" % _s, "h_%d" % _s, "q_%d" % _s, "mm%da" % _s, "mm%db" % _s, "d_%d" % _s]
+    SEMAPHORES += ["a_%d_%d" % (_s, _t) for _t in range(4)]
+for _b in range(8):
+    SCRATCH["ps%d" % _b] = ("psum", [128, 512], "float32")
+
+
+def kind_of(src, dst, cores, topo):
+    a, b = topo.chip(cores[src]), topo.chip(cores[dst])
+    if topo.mates(a, b):
+        return "mate"
+    if topo.same_plane(a, b):
+        ring = [s for s in range(N) if s == src or topo.same_plane(a, topo.chip(cores[s]))]
+        return "next" if ring[(ring.index(src) + 1) % len(ring)] == dst else "plane"
+    return "far"
+
+
+def rank_program(g, core, T, topo):
+    r = T.rank_of(core)
+    if r is None:
+        return
+    cores = list(T.cores)
+    S = T.sem
+    others = [(r + i) % N for i in range(1, N)]
+    to = {s: kind_of(r, s, cores, topo) for s in others}
+    frm = {s: kind_of(s, r, cores, topo) for s in others}
+    code_dst = [s for k in ("next", "mate") for s in others if to[s] == k]
+    list_dst = [s for k in ("far", "plane") for s in others if to[s] == k]
+    lists = [s for k in ("plane", "far") for s in others if frm[s] == k]
+    mate = [s for s in others if frm[s] == "mate"]
+    nxt = [s for s in others if frm[s] == "next"]
+    made = [r] + lists
+    order = [r] + lists[:-1] + mate + lists[-1:] + nxt
+    half = 4 * P // 16
+
+    g.sync.dma_start(T.cwb[:], T.cw[:]).then_inc(S.l_cw, 16)
+    g.sync.dma_start(T.b0[:], T.book[:, 0:4 * K]).then_inc(S.l_b0, 16)
+    g.sync.dma_start(T.b1[:], T.book[:, 4 * K:8 * K]).then_inc(S.l_b1, 16)
+    g.sync.dma_start(T.xb[:], T.x[:]).then_inc(S.l_x, 16)
+
+    def offs(s):
+        return T.of if s == r else T["L%d" % s]
+
+    v = g.vector
+    v.wait_ge(S.l_cw, 16)
+    for m in range(2):
+        for t in range(4):
+            c = m * half + t * (P // 16)
+            v.tensor_scalar(T.of[:, c:c + P // 16], T.cwb[:, :, m, :], 4, t, AluOpType.mult, AluOpType.add).then_inc(S["ofb" if m else "ofa"], 1)
+    v.wait_ge(S.ofb, 4)
+    v.wait_ge(S.ofa, 4)
+    v.wait_ge(S.l_b0, 16)
+    v.wait_ge(S.l_b1, 16)
+
+    def add(s, t):
+        if s != r and t == 0:
+            v.wait_ge(S["arrl%d" % s], len(topo.engines(cores[s], core)))
+        if s == r or t == 0:
+            v.wait_ge(S["a_%d_%d" % (s, t)], 1)
+        c = half + t * (P // 16)
+        v.tensor_tensor(T["h%d" % s][:, t:4 * P:4], T.b1[:, 0:4 * K].indirect(offs(s)[:, c:c + P // 16]),
+                        T["a%d" % s][:, t * P:(t + 1) * P], AluOpType.add).then_inc(S["h_%d" % s], 1)
+
+    def pack(s):
+        v.wait_ge(S["h_%d" % s], 4)
+        v.quantize_mx(T["q%d" % s][:, 0:P], T["p%d" % s][:, 0:P], T["h%d" % s][:, 0:4 * P]).then_inc(S["q_%d" % s], 1)
+
+    for t in range(4):
+        add(r, t)
+    v.wait_ge(S.l_x, 16)
+    v.quantize_mx(T.qx[:, 0:W], T.px[:, 0:W], T.xb[:, 0:4 * W]).then_inc(S.v_qx, 1)
+    pack(r)
+    for i, s in enumerate(lists):
+        for t in range(4):
+            add(s, t)
+            if t == 0 and i:
+                pack(lists[i - 1])
+    pack(lists[-1])
+
+    sc = g.scalar
+    copy = ActivationFunctionType.Copy
+
+    def drain(eng, s, o):
+        src = T["ps%d" % ((2 * order.index(s) + o) % 8)][:, 0:W]
+        dst = T.yb[:, s * P + o * W:s * P + (o + 1) * W]
+        eng.wait_ge(S["mm%d%s" % (s, "ab"[o])], 1)
+        ins = sc.activation(dst, src, copy) if eng is sc else v.tensor_copy(dst, src)
+        ins.then_inc(S["d_%d" % s], 1)
+
+    sc.wait_ge(S.ofa, 4)
+    sc.wait_ge(S.l_b0, 16)
+    for i, s in enumerate(made):
+        w = offs(s)
+        if s == r:
+            for t in range(4):
+                c = t * (P // 16)
+                sc.activation(T["a%d" % s][:, t * P:(t + 1) * P], T.b0[:, 0:4 * K].indirect(w[:, c:c + P // 16]), copy).then_inc(S["a_%d_%d" % (s, t)], 1)
+        else:
+            sc.wait_ge(S["arrl%d" % s], len(topo.engines(cores[s], core)))
+            sc.activation(T["a%d" % s][:, 0:4 * P], T.b0[:, 0:4 * K].indirect(w[:, 0:half]), copy).then_inc(S["a_%d_0" % s], 1)
+        if i == len(made) - 2:
+            drain(sc, r, 0)
+            drain(sc, r, 1)
+    late = order[order.index(lists[-1]):]
+    for s in order[1:]:
+        drain(sc, s, 0)
+        drain(v if s in late else sc, s, 1)
+
+    g.tensor.wait_ge(S.v_qx, 1)
+    for i, s in enumerate(order):
+        if s in made:
+            g.tensor.wait_ge(S["q_%d" % s], 1)
+        else:
+            g.tensor.wait_ge(S["arrc%d" % s], 2 * len(topo.engines(cores[s], core)))
+        if i >= 4:
+            g.tensor.wait_ge(S["d_%d" % order[i - 4]], 2)
+        for o in range(O):
+            q, p = T["q%d" % s], T["p%d" % s]
+            g.tensor.matmul_mx(T["ps%d" % ((2 * i + o) % 8)][:, 0:W], q[:, o * W:(o + 1) * W], p[:, o * W:(o + 1) * W],
+                               T.qx[:, 0:W], T.px[:, 0:W], True, True).then_inc(S["mm%d%s" % (s, "ab"[o])], 1)
+
+    for s in order:
+        g.sync.wait_ge(S["d_%d" % s], 2)
+        g.sync.dma_start(T.y[:, s * P:(s + 1) * P], T.yb[:, s * P:(s + 1) * P]).then_inc(S.stored, 16)
+    g.sync.wait_ge(S.stored, 16 * N)
+
+    def send(dsts, src, dst, sem, done):
+        ids = []
+        for d in dsts:
+            rid, pid, _ = topo.addr(cores[d])
+            ids.append(DstId(rid=rid, pnc=pid))
+        m = topo.mask(core, cores[dsts[0]])
+        g.remote_dma_fused([RemoteDMATransfer(dst_ids=ids, dma_engine_mask=m, remote_sem=sem, srcs=[src], dsts=[dst] * len(dsts))], local_sem=done)
+
+    eng = len(topo.engines(core, cores[list_dst[0]]))
+    g.wait_ge(S.ofa, 4)
+    g.wait_ge(S.ofb, 4)
+    send(list_dst, T.of[:], T["L%d" % r][:], S["arrl%d" % r], S.sent_l)
+    g.wait_ge(S["q_%d" % r], 1)
+    q, p = T["q%d" % r], T["p%d" % r]
+    send(code_dst, q[:, 0:P].bitcast(dt.uint8), q[:, 0:P].bitcast(dt.uint8), S["arrc%d" % r], S.sent_c)
+    send(code_dst, p[:, 0:P], p[:, 0:P], S["arrc%d" % r], S.sent_c)
+    g.wait_ge(S.sent_l, eng)
+    g.wait_ge(S.sent_c, 2 * eng)

@@ -21,7 +21,7 @@ for _s in range(N):
     SCRATCH["h%d" % _s] = ("sbuf", [128, 4 * P], "bfloat16")
     SCRATCH["q%d" % _s] = ("sbuf", [128, P], "float8_e4m3fn_x4")
     SCRATCH["p%d" % _s] = ("sbuf", [128, P], "uint8")
-    SEMAPHORES += ["arrl%d" % _s, "arrc%d" % _s, "h_%d" % _s, "q_%d" % _s, "mm%da" % _s, "mm%db" % _s, "d_%d" % _s]
+    SEMAPHORES += ["arrl%d" % _s, "arrc%d" % _s, "h_%d" % _s, "q_%da" % _s, "q_%db" % _s, "mm%da" % _s, "mm%db" % _s, "d_%d" % _s]
     SEMAPHORES += ["a_%d_%d" % (_s, _t) for _t in range(4)]
 for _b in range(8):
     SCRATCH["ps%d" % _b] = ("psum", [128, 512], "float32")
@@ -43,16 +43,17 @@ def rank_program(g, core, T, topo):
         return
     cores = list(T.cores)
     S = T.sem
-    others = [(r + i) % N for i in range(1, N)]
-    to = {s: kind_of(r, s, cores, topo) for s in others}
-    frm = {s: kind_of(s, r, cores, topo) for s in others}
-    code_dst = [s for k in ("next", "mate") for s in others if to[s] == k]
-    list_dst = [s for k in ("far", "plane") for s in others if to[s] == k]
-    lists = [s for k in ("plane", "far") for s in others if frm[s] == k]
-    mate = [s for s in others if frm[s] == "mate"]
-    nxt = [s for s in others if frm[s] == "next"]
+    ups = [(r + i) % N for i in range(1, N)]
+    downs = [(r - i) % N for i in range(1, N)]
+    to = {s: kind_of(r, s, cores, topo) for s in ups}
+    frm = {s: kind_of(s, r, cores, topo) for s in ups}
+    code_dst = [s for k in ("next", "mate") for s in ups if to[s] == k]
+    list_dst = [s for k in ("plane", "far") for s in ups if to[s] == k]
+    lists = [s for k in ("plane", "far") for s in downs if frm[s] == k]
+    mate = [s for s in ups if frm[s] == "mate"]
+    nxt = [s for s in ups if frm[s] == "next"]
     made = [r] + lists
-    order = [r] + lists[:-1] + mate + lists[-1:] + nxt
+    order = [r] + lists[:-1] + mate + nxt + lists[-1:]
     half = 4 * P // 16
 
     g.sync.dma_start(T.cwb[:], T.cw[:]).then_inc(S.l_cw, 16)
@@ -77,21 +78,25 @@ def rank_program(g, core, T, topo):
     def add(s, t):
         if s != r and t == 0:
             v.wait_ge(S["arrl%d" % s], len(topo.engines(cores[s], core)))
-        if s == r or t == 0:
-            v.wait_ge(S["a_%d_%d" % (s, t)], 1)
+        v.wait_ge(S["a_%d_%d" % (s, t)], 1)
         c = half + t * (P // 16)
         v.tensor_tensor(T["h%d" % s][:, t:4 * P:4], T.b1[:, 0:4 * K].indirect(offs(s)[:, c:c + P // 16]),
                         T["a%d" % s][:, t * P:(t + 1) * P], AluOpType.add).then_inc(S["h_%d" % s], 1)
 
     def pack(s):
         v.wait_ge(S["h_%d" % s], 4)
-        v.quantize_mx(T["q%d" % s][:, 0:P], T["p%d" % s][:, 0:P], T["h%d" % s][:, 0:4 * P]).then_inc(S["q_%d" % s], 1)
+        if s == lists[-1]:
+            for o in range(O):
+                v.quantize_mx(T["q%d" % s][:, o * W:(o + 1) * W], T["p%d" % s][:, o * W:(o + 1) * W],
+                              T["h%d" % s][:, 4 * o * W:4 * (o + 1) * W]).then_inc(S["q_%d%s" % (s, "ab"[o])], 1)
+        else:
+            v.quantize_mx(T["q%d" % s][:, 0:P], T["p%d" % s][:, 0:P], T["h%d" % s][:, 0:4 * P]).then_inc(S["q_%da" % s], 1)
 
     for t in range(4):
         add(r, t)
+    pack(r)
     v.wait_ge(S.l_x, 16)
     v.quantize_mx(T.qx[:, 0:W], T.px[:, 0:W], T.xb[:, 0:4 * W]).then_inc(S.v_qx, 1)
-    pack(r)
     for i, s in enumerate(lists):
         for t in range(4):
             add(s, t)
@@ -112,31 +117,29 @@ def rank_program(g, core, T, topo):
     sc.wait_ge(S.ofa, 4)
     sc.wait_ge(S.l_b0, 16)
     for i, s in enumerate(made):
-        w = offs(s)
-        if s == r:
-            for t in range(4):
-                c = t * (P // 16)
-                sc.activation(T["a%d" % s][:, t * P:(t + 1) * P], T.b0[:, 0:4 * K].indirect(w[:, c:c + P // 16]), copy).then_inc(S["a_%d_%d" % (s, t)], 1)
-        else:
+        if s != r:
             sc.wait_ge(S["arrl%d" % s], len(topo.engines(cores[s], core)))
-            sc.activation(T["a%d" % s][:, 0:4 * P], T.b0[:, 0:4 * K].indirect(w[:, 0:half]), copy).then_inc(S["a_%d_0" % s], 1)
+        for t in range(4):
+            c = t * (P // 16)
+            sc.activation(T["a%d" % s][:, t * P:(t + 1) * P], T.b0[:, 0:4 * K].indirect(offs(s)[:, c:c + P // 16]), copy).then_inc(S["a_%d_%d" % (s, t)], 1)
         if i == len(made) - 2:
             drain(sc, r, 0)
             drain(sc, r, 1)
-    late = order[order.index(lists[-1]):]
     for s in order[1:]:
         drain(sc, s, 0)
-        drain(v if s in late else sc, s, 1)
+        drain(v if s == order[-1] else sc, s, 1)
 
     g.tensor.wait_ge(S.v_qx, 1)
     for i, s in enumerate(order):
         if s in made:
-            g.tensor.wait_ge(S["q_%d" % s], 1)
+            g.tensor.wait_ge(S["q_%da" % s], 1)
         else:
             g.tensor.wait_ge(S["arrc%d" % s], 2 * len(topo.engines(cores[s], core)))
         if i >= 4:
             g.tensor.wait_ge(S["d_%d" % order[i - 4]], 2)
         for o in range(O):
+            if o and s == lists[-1]:
+                g.tensor.wait_ge(S["q_%db" % s], 1)
             q, p = T["q%d" % s], T["p%d" % s]
             g.tensor.matmul_mx(T["ps%d" % ((2 * i + o) % 8)][:, 0:W], q[:, o * W:(o + 1) * W], p[:, o * W:(o + 1) * W],
                                T.qx[:, 0:W], T.px[:, 0:W], True, True).then_inc(S["mm%d%s" % (s, "ab"[o])], 1)
@@ -158,7 +161,7 @@ def rank_program(g, core, T, topo):
     g.wait_ge(S.ofa, 4)
     g.wait_ge(S.ofb, 4)
     send(list_dst, T.of[:], T["L%d" % r][:], S["arrl%d" % r], S.sent_l)
-    g.wait_ge(S["q_%d" % r], 1)
+    g.wait_ge(S["q_%da" % r], 1)
     q, p = T["q%d" % r], T["p%d" % r]
     send(code_dst, q[:, 0:P].bitcast(dt.uint8), q[:, 0:P].bitcast(dt.uint8), S["arrc%d" % r], S.sent_c)
     send(code_dst, p[:, 0:P], p[:, 0:P], S["arrc%d" % r], S.sent_c)

from concourse.bass import DstId, RemoteDMATransfer
from concourse.mybir import dt, AluOpType, ActivationFunctionType

N, O, W, K = 6, 2, 128, 256
P = O * W

SCRATCH = {
    "cwb": ("sbuf", [128, O, 2, W // 16], "int32"),
    "b0": ("sbuf", [128, 4 * K], "bfloat16"),
    "b1": ("sbuf", [128, 4 * K], "bfloat16"),
    "xb": ("sbuf", [128, 4 * W], "bfloat16"),
    "qx": ("sbuf", [128, W], "float8_e4m3fn_x4"),
    "px": ("sbuf", [128, W], "uint8"),
    "of": ("sbuf", [128, 2 * 4 * P // 16], "uint16"),
    "yb": ("sbuf", [128, N * P], "float32"),
}
SEMAPHORES = ["l_cw", "l_b0", "l_b1", "l_x", "ofa", "ofb", "v_qx", "sent_l", "sent_c", "stored"]
for _s in range(N):
    SCRATCH["L%d" % _s] = ("sbuf", [128, 2 * 4 * P // 16], "uint16")
    SCRATCH["a%d" % _s] = ("sbuf", [128, 4 * P], "bfloat16")
    SCRATCH["h%d" % _s] = ("sbuf", [128, 4 * P], "bfloat16")
    SCRATCH["q%d" % _s] = ("sbuf", [128, P], "float8_e4m3fn_x4")
    SCRATCH["p%d" % _s] = ("sbuf", [128, P], "uint8")
    SEMAPHORES += ["arrl%d" % _s, "arrc%d" % _s, "h_%d" % _s, "q_%da" % _s, "q_%db" % _s, "mm%da" % _s, "mm%db" % _s, "d_%d" % _s]
    SEMAPHORES += ["a_%d_%d" % (_s, _t) for _t in range(4)]
for _b in range(8):
    SCRATCH["ps%d" % _b] = ("psum", [128, 512], "float32")


def kind_of(src, dst, cores, topo):
    a, b = topo.chip(cores[src]), topo.chip(cores[dst])
    if topo.mates(a, b):
        return "mate"
    if topo.same_plane(a, b):
        ring = [s for s in range(N) if s == src or topo.same_plane(a, topo.chip(cores[s]))]
        return "next" if ring[(ring.index(src) + 1) % len(ring)] == dst else "plane"
    return "far"


def rank_program(g, core, T, topo):
    r = T.rank_of(core)
    if r is None:
        return
    cores = list(T.cores)
    S = T.sem
    ups = [(r + i) % N for i in range(1, N)]
    downs = [(r - i) % N for i in range(1, N)]
    to = {s: kind_of(r, s, cores, topo) for s in ups}
    frm = {s: kind_of(s, r, cores, topo) for s in ups}
    code_dst = [s for k in ("next", "mate") for s in ups if to[s] == k]
    list_dst = [s for k in ("plane", "far") for s in ups if to[s] == k]
    lists = [s for k in ("plane", "far") for s in downs if frm[s] == k]
    mate = [s for s in ups if frm[s] == "mate"]
    nxt = [s for s in ups if frm[s] == "next"]
    made = [r] + lists
    order = [r] + lists[:-1] + mate + nxt + lists[-1:]
    half = 4 * P // 16

    g.sync.dma_start(T.cwb[:], T.cw[:]).then_inc(S.l_cw, 16)
    g.sync.dma_start(T.b0[:], T.book[:, 0:4 * K]).then_inc(S.l_b0, 16)
    g.sync.dma_start(T.b1[:], T.book[:, 4 * K:8 * K]).then_inc(S.l_b1, 16)
    g.sync.dma_start(T.xb[:], T.x[:]).then_inc(S.l_x, 16)

    def offs(s):
        return T.of if s == r else T["L%d" % s]

    v = g.vector
    v.wait_ge(S.l_cw, 16)
    for m in range(2):
        for t in range(4):
            c = m * half + t * (P // 16)
            v.tensor_scalar(T.of[:, c:c + P // 16], T.cwb[:, :, m, :], 4, t, AluOpType.mult, AluOpType.add).then_inc(S["ofb" if m else "ofa"], 1)
    v.wait_ge(S.ofb, 4)
    v.wait_ge(S.ofa, 4)
    v.wait_ge(S.l_b0, 16)
    v.wait_ge(S.l_b1, 16)

    def add(s, t):
        if s != r and t == 0:
            v.wait_ge(S["arrl%d" % s], len(topo.engines(cores[s], core)))
        v.wait_ge(S["a_%d_%d" % (s, t)], 1)
        c = half + t * (P // 16)
        v.tensor_tensor(T["h%d" % s][:, t:4 * P:4], T.b1[:, 0:4 * K].indirect(offs(s)[:, c:c + P // 16]),
                        T["a%d" % s][:, t * P:(t + 1) * P], AluOpType.add).then_inc(S["h_%d" % s], 1)

    def pack(s):
        v.wait_ge(S["h_%d" % s], 4)
        if s == lists[-1]:
            for o in range(O):
                v.quantize_mx(T["q%d" % s][:, o * W:(o + 1) * W], T["p%d" % s][:, o * W:(o + 1) * W],
                              T["h%d" % s][:, 4 * o * W:4 * (o + 1) * W]).then_inc(S["q_%d%s" % (s, "ab"[o])], 1)
        else:
            v.quantize_mx(T["q%d" % s][:, 0:P], T["p%d" % s][:, 0:P], T["h%d" % s][:, 0:4 * P]).then_inc(S["q_%da" % s], 1)

    for t in range(4):
        add(r, t)
    pack(r)
    v.wait_ge(S.l_x, 16)
    v.quantize_mx(T.qx[:, 0:W], T.px[:, 0:W], T.xb[:, 0:4 * W]).then_inc(S.v_qx, 1)
    for i, s in enumerate(lists):
        for t in range(4):
            add(s, t)
            if t == 0 and i:
                pack(lists[i - 1])
    pack(lists[-1])

    sc = g.scalar
    copy = ActivationFunctionType.Copy

    def drain(eng, s, o):
        src = T["ps%d" % ((2 * order.index(s) + o) % 8)][:, 0:W]
        dst = T.yb[:, s * P + o * W:s * P + (o + 1) * W]
        eng.wait_ge(S["mm%d%s" % (s, "ab"[o])], 1)
        ins = sc.activation(dst, src, copy) if eng is sc else v.tensor_copy(dst, src)
        ins.then_inc(S["d_%d" % s], 1)

    sc.wait_ge(S.ofa, 4)
    sc.wait_ge(S.l_b0, 16)
    for i, s in enumerate(made):
        if s != r:
            sc.wait_ge(S["arrl%d" % s], len(topo.engines(cores[s], core)))
        for t in range(4):
            c = t * (P // 16)
            sc.activation(T["a%d" % s][:, t * P:(t + 1) * P], T.b0[:, 0:4 * K].indirect(offs(s)[:, c:c + P // 16]), copy).then_inc(S["a_%d_%d" % (s, t)], 1)
        if i == len(made) - 2:
            drain(sc, r, 0)
            drain(sc, r, 1)
    for s in order[1:]:
        drain(sc, s, 0)
        drain(v if s == order[-1] else sc, s, 1)

    g.tensor.wait_ge(S.v_qx, 1)
    for i, s in enumerate(order):
        if s in made:
            g.tensor.wait_ge(S["q_%da" % s], 1)
        else:
            g.tensor.wait_ge(S["arrc%d" % s], 2 * len(topo.engines(cores[s], core)))
        if i >= 4:
            g.tensor.wait_ge(S["d_%d" % order[i - 4]], 2)
        for o in range(O):
            if o and s == lists[-1]:
                g.tensor.wait_ge(S["q_%db" % s], 1)
            q, p = T["q%d" % s], T["p%d" % s]
            g.tensor.matmul_mx(T["ps%d" % ((2 * i + o) % 8)][:, 0:W], q[:, o * W:(o + 1) * W], p[:, o * W:(o + 1) * W],
                               T.qx[:, 0:W], T.px[:, 0:W], True, True).then_inc(S["mm%d%s" % (s, "ab"[o])], 1)

    for s in order:
        g.sync.wait_ge(S["d_%d" % s], 2)
        g.sync.dma_start(T.y[:, s * P:(s + 1) * P], T.yb[:, s * P:(s + 1) * P]).then_inc(S.stored, 16)
    g.sync.wait_ge(S.stored, 16 * N)

    def send(dsts, src, dst, sem, done):
        ids = []
        for d in dsts:
            rid, pid, _ = topo.addr(cores[d])
            ids.append(DstId(rid=rid, pnc=pid))
        m = topo.mask(core, cores[dsts[0]])
        g.remote_dma_fused([RemoteDMATransfer(dst_ids=ids, dma_engine_mask=m, remote_sem=sem, srcs=[src], dsts=[dst] * len(dsts))], local_sem=done)

    eng = len(topo.engines(core, cores[list_dst[0]]))
    g.wait_ge(S.ofa, 4)
    g.wait_ge(S.ofb, 4)
    send(list_dst, T.of[:], T["L%d" % r][:], S["arrl%d" % r], S.sent_l)
    g.wait_ge(S["q_%da" % r], 1)
    q, p = T["q%d" % r], T["p%d" % r]
    send(code_dst, q[:, 0:P].bitcast(dt.uint8), q[:, 0:P].bitcast(dt.uint8), S["arrc%d" % r], S.sent_c)
    send(code_dst, p[:, 0:P], p[:, 0:P], S["arrc%d" % r], S.sent_c)
    g.wait_ge(S.sent_l, eng)
    g.wait_ge(S.sent_c, 2 * eng)
